import numpy as np, ml_dtypes
CORES = [10,34,74,98]
N = 4
BF = ml_dtypes.bfloat16
W, C, RU, S, M = 8192, 128, 3, 4, 7
def bf(x):
    return np.ascontiguousarray(x).astype(np.float32).astype(BF)
def parts(rng):
    d = {"ends": rng.integers(0, 256, (N, 8, 16, C)), "db": rng.integers(0, 256, (N, 8, 16, W), dtype=np.int16)}
    d["db"][:, :, 15] = rng.integers(0, M + 1, (N, 8, W)) * (rng.random((N, 8, W)) < 0.75)
    d["wt"] = rng.integers(0, rng.choice(np.array([2, 6, 12, 18]), (N, 8, 1, 16)), (N, 8, 16, 16))
    d["salt"] = rng.integers(0, W, (N, 8, 16, C)); d["nz"] = rng.integers(0, 256, (N, 8, 16, RU, S, C))
    k = rng.random((N, 8, RU, C))
    d["sl"] = np.where(k < 0.0625, 4000, np.where(k > 0.9375, -4000, rng.integers(-700, 401, (N, 8, RU, C))))
    return d
def pack(d):
    for k in ("ends", "wt", "nz"): d[k][:, :, 15] = 0
    return {"ends": bf(d["ends"].reshape(N, 128, C)), "db": bf(d["db"].reshape(N, 128, W)), "wt": bf(d["wt"].reshape(N, 128, 16)),
            "salt": np.ascontiguousarray(d["salt"].reshape(N, 128, C)).astype(np.int32), "nz": bf(d["nz"].reshape(N, 128, RU * S * C)),
            "sl": np.ascontiguousarray(d["sl"].reshape(N, 8, RU * C)).astype(np.int32)}
def walk(e, D, wt, salt, nz, sl, delta=None):
    e = e.astype(np.int32); D = D.astype(np.int32); w = wt.astype(np.int32).transpose(0, 1, 3, 2); a = salt.astype(np.int32); z = nz.astype(np.int32)
    verdicts, places = [], []
    for m in range(RU):
        v = np.roll(e, 1, axis=0); t = np.roll(e, -1, axis=0)
        shadow = []
        for s in range(S):
            u = np.matmul(w, v) >> 6
            pl = ((u * u >> 3) + 37 * u + 211 * s + a) & (W - 1)
            got = np.take_along_axis(D, pl.transpose(0, 1, 3, 2).reshape(N, 8, 1, C * 16), 3).reshape(N, 8, 16, C, 16)
            ask = (u & M).transpose(0, 1, 3, 2)
            hit = (got[:, :, 15] == ask) & (((np.arange(C) + m) & 3) != s)[:, None]
            f = (v + z[:, :, :, m, s]) & 255
            x = np.where(hit[:, :, None], got, f[..., None])
            first = np.argmin(hit, axis=3)
            place = np.take_along_axis(pl, first[:, :, None, :], 2)[:, :, 0]
            rec = f + 0; rec[:, :, 15] = np.take_along_axis(ask, first[..., None], 3)[..., 0]
            place = np.where(np.all(hit, axis=3), -1, place)
            shadow.append((place, rec)); places.append(place)
            v = (2 * v + np.max(x, axis=4) + np.min(x, axis=4)) >> 2; v[:, :, 15] = 0
        A = np.sum(np.abs(v - t), axis=2); B = np.sum(np.abs(e - t), axis=2)
        if delta is not None: sl[:, :, m] = A - B + delta[:, :, m]
        ok = A <= B + sl[:, :, m]
        e = np.where(ok[:, :, None], v, e); verdicts.append(ok)
        for place, rec in shadow:
            for q in range(N):
                for g in range(8):
                    c = np.flatnonzero(ok[q, g] & (place[q, g] >= 0))
                    to, at = np.unique(place[q, g, c], return_index=True)
                    D[q, g][:, to] = rec[q, g][:, c[at]]
    return e, np.stack(verdicts, 2), np.stack(places, 2)
def setup_inputs(rng):
    return pack(parts(rng))
def setup_inputs_again(rng):
    d = parts(rng)
    turn = (np.arange(N)[:, None, None, None] + np.arange(8)[:, None, None] + np.arange(RU)[:, None]) & 1
    d["sl"] = np.where(rng.random((N, 8, RU, C)) < 0.875, np.where(turn == 1, 4000, -4000), d["sl"])
    return pack(d)
def setup_inputs_alike(rng):
    d = parts(rng); c = np.arange(C)
    d["wt"][:, :3] = 0
    d["salt"][:, :3] = (rng.integers(0, W, (N, 3, 16, 1)) + 211 * (c & 3) * (np.arange(3)[:, None, None] > 0)) & (W - 1)
    d["db"][::2, 0, 15] = rng.integers(1, M + 1, d["db"][::2, 0, 15].shape); d["sl"][::2, 0, 0] = 4000
    ix = rng.integers(0, 4, C)
    d["ends"][:, 3:6] = d["ends"][:, 3:6][..., ix]; d["salt"][:, 3:6] = d["salt"][:, 3:6][..., ix]
    d["wt"][:, 6] = d["wt"][:, 6][:, :, :1] + np.zeros((1, 1, 16), np.int64); d["salt"][:, 6] = d["salt"][:, 6][:, :1] + np.zeros((1, 16, 1), np.int64)
    d["wt"][:, 7] = 0; d["db"][:, 7, 15] = rng.integers(1, M + 1, (N, W))
    x = 8 * np.argsort(rng.random((N, W // 8)), axis=1)[:, :C]
    for p in range(4):
        d["salt"][:, 7, p] = (x - 211 * p) & (W - 1)
        for q in range(N):
            if p > 0: d["db"][q, 7, 15, (x[q] + 211 * p) & (W - 1)] = 0
    d["sl"][:, 7] = np.where(rng.random((N, RU, C)) < 0.75, 4000, d["sl"][:, 7])
    return pack(d)
def setup_inputs_full(rng):
    d = parts(rng); c = np.arange(C)
    d["wt"][:, 0] = 0; d["db"][:, 0, 15] = 0
    d["wt"][:, 1] = 0; d["db"][:, 1, 15] = rng.integers(1, M + 1, (N, W))
    d["wt"][:, 2] = 0; d["wt"][:, 2, :, 15] = rng.integers(1, 18, (N, 16)); d["db"][:, 2, 15] = 0
    d["wt"][:, 3] = 17; d["ends"][:, 3, :, c % 2 == 0] = 255; d["nz"][:, 3, :, :, :, c % 2 == 0] = 0
    d["db"][:, 3, :15] = 255 - rng.integers(0, 5, (N, 15, W)) * (np.arange(N) & 1)[:, None, None]
    d["db"][:, 4, :15] = 255 * rng.integers(0, 2, (N, 15, W)); d["ends"][:, 4] = 255 * rng.integers(0, 2, (N, 16, C))
    d["ends"][:, 5, :, c % 2 == 0] = 0; d["nz"][:, 5, :, :, :, c % 2 == 0] = 0
    d["salt"][:, :2] = np.where(rng.random((N, 2, 16, C)) < 0.5, (W - 1) * rng.integers(0, 2, (N, 2, 16, C)), d["salt"][:, :2])
    d["salt"][:, 0, 0] = (W - 1) * (((c >> 2) + np.arange(N)[:, None]) & 1)
    d["wt"][:, 6] = 0; d["db"][:, 6, 15] = rng.integers(1, M + 1, (N, W))
    d["salt"][:, 6, 0] = 8 * np.argsort(rng.random((N, W // 8)), axis=1)[:, :C] + rng.integers(0, 8, (N, 1))
    d["sl"][:, 6, 0] = np.where((np.arange(N) & 1) == 0, 4000, -4000)[:, None]
    return pack(d)
def setup_inputs_ties(rng):
    d = parts(rng); r = np.arange(N)
    d["ends"][:, 0] = 0; d["nz"][:, 0] = 0; d["db"][:, 0, :15] = 0
    for g, b in ((1, (r >> 1) & 1), (2, r & 1)):
        b = b[:, None, None]
        d["ends"][:, g] = np.abs(255 * b - rng.integers(0, 16, (N, 16, C))); d["nz"][:, g] = 0
        d["db"][:, g, :15] = np.abs(255 * np.roll(b, 1, axis=0) - rng.integers(0, 16, (N, 15, W)))
    for k in ("ends", "wt", "nz"): d[k][:, :, 15] = 0
    walk(d["ends"], d["db"], d["wt"], d["salt"], d["nz"], d["sl"], rng.integers(-1, 2, (N, 8, RU, C)))
    return pack(d)
def setup_inputs_spread(rng):
    d = parts(rng)
    d["ends"] = (np.exp2(8 * rng.random((N, 8, 1, C))) * rng.random((N, 8, 16, C))).astype(np.int64)
    d["nz"] = (np.exp2(8 * rng.random((N, 8, 1, RU, S, C))) * rng.random((N, 8, 16, RU, S, C))).astype(np.int64)
    d["db"] = (np.exp2(8 * rng.random((N, 8, 1, W))) * rng.random((N, 8, 16, W))).astype(np.int16)
    d["db"][:, :, 15] = np.minimum((M + 1) * rng.random((N, 8, W)) ** rng.choice(np.array([0.5, 1.0, 3.0]), (N, 8, 1)), M).astype(np.int16)
    d["wt"] = np.minimum((np.exp2(4.2 * rng.random((N, 8, 1, 16))) * rng.random((N, 8, 16, 16))).astype(np.int64), 17)
    d["sl"] = rng.integers(-4000, 4001, (N, 8, RU, C))
    return pack(d)
def check_inputs(d):
    bad = []
    for k, lo, hi in (("ends", 0, 255), ("db", 0, 255), ("wt", 0, 17), ("salt", 0, W - 1), ("nz", 0, 255), ("sl", -4000, 4000)):
        x = np.asarray(d[k]).astype(np.float64)
        if not (np.min(x) >= lo and np.max(x) <= hi): bad.append("range of " + k)
        elif np.any(x != np.floor(x)): bad.append("whole numbers in " + k)
    for k, hi in (("ends", 0), ("wt", 0), ("nz", 0), ("db", M)):
        x = np.asarray(d[k]).astype(np.float64).reshape(N, 8, 16, -1)[:, :, 15]
        if not np.max(x) <= hi: bad.append("rows 16*g + 15 of " + k)
    return bad
def reference(ends, db, wt, salt, nz, sl):
    h = [x.astype(np.float32).astype(np.int32) for x in (ends, db, wt, nz)]
    e, ok, place = walk(h[0].reshape(N, 8, 16, C), h[1].reshape(N, 8, 16, W), h[2].reshape(N, 8, 16, 16), salt.reshape(N, 8, 16, C), h[3].reshape(N, 8, 16, RU, S, C), sl.astype(np.int64).reshape(N, 8, RU, C))
    return {"ye": e.reshape(N, 128, C).astype(np.float32).astype(BF), "yv": ok.reshape(N, 8, RU * C).astype(np.float32), "yp": place.reshape(N, 8, RU * S * C).astype(np.float32)}

import numpy as np
from concourse.mybir import AluOpType, ActivationFunctionType

A = AluOpType
AF = ActivationFunctionType

NS = 2
NB = 128 // NS
B = NB // 4
AC = 3 * B
W = 8192
FB = W + 128
WC = FB + 12 * 128
PARAM = {"g": 1.56, "sc": 4.0, "pe": 0.5, "db": 8000.0, "rem": 3000.0, "hop": 100.0, "delta": 60.0,
         "gv": [[18, 14], [18, 14]], "ea": 1, "skew": 1000.0, "off": -1500.0, "lift": 2500.0,
         "few": 1200, "many": 9000, "heat": 60.0,
         "cases": [{"g": 1.4, "sc": 3.0, "hop": 60.0, "pe": 0.5, "fix": 0},
                   {"g": 1.7, "sc": 4.5, "hop": 130.0, "pe": 0.6, "fix": 30}]}
TRY = [{"gv": [a, b], "ea": f, "skew": k}
       for (a, b, f) in (([18, 14], [18, 14], 1), ([14, 10], [16, 12], 0), ([16, 12], [18, 14], 1), ([16, 14], [20, 16], 1))
       for k in (700.0, 1000.0, 1400.0)]
LIFT = {"ee", "okf", "prod", "aA", "x2", "ofs", "okT"}

S_, F_, I_, U_ = "bfloat16", "float32", "int32", "uint16"
SCRATCH = {"sd": ("sbuf", [128, NS, 8, B], F_), "sd8": ("sbuf", [128, 4 * NS, 8, B], F_),
           "ask": ("sbuf", [128, 4 * NS, NB], I_), "d1": ("sbuf", [128, 12 * NS, 2 * NB], F_),
           "fi": ("sbuf", [128, 4 * NS, NB], S_)}
for _d, _l in ((S_, {"win": WC, "e_in": 128, "wt_in": 16, "nz_in": 1536, "ee": 512, "e0": 128, "vin": 384, "tin": 384,
                     "vv": 1536, "mI": 128, "mIn": 128, "mI128": 128, "mIb": 128, "mIc": 128, "mH4": 128, "mF2": 128,
                     "mV2": 128, "mBO": 128, "mT": 144, "mL": 128, "mR15": 128, "mR": 512, "mRR": 128, "mY": 128,
                     "mTri": 256, "mW": 128, "wt2": 16, "ones": 128, "rs0": 16 * AC, "rs1": 16 * AC, "got": 3072,
                     "xx": 3072, "smx": 3072, "smn": 3072, "d0": 384, "mb": 256, "pA": 256, "rec": 512, "gg": 256,
                     "ff": 512, "eq": 1024, "aA": 128, "aB": 128, "okT": 128, "prod": 128}),
               (F_, {"slf": 384, "nN": 128, "nG": 128, "nI": 128, "col": 20, "gcol": 8, "rcol": 16, "n8": 8, "n32": 32,
                     "nJ": 256, "mBf": 128, "mYf": 128, "mTr": 128, "mA": 8, "mG": 128, "tmp": 512, "uu": 256,
                     "o2": 384, "pP": 512, "bs": 128, "bsT": 128, "okf": 384, "x2": 512, "ypa": 128, "ypb": 384}),
               (I_, {"salt_in": 128, "sl_in": 384, "pk": 4, "zz": 256, "pl": 256, "ui": 256}),
               (U_, {"of1": 192, "of2": 192, "ofs": 32})):
    for _k in _l:
        SCRATCH[_k] = ("sbuf", [128, _l[_k]], _d)
for _b in range(8):
    SCRATCH["ps%d" % _b] = ("psum", [128, 512], F_)
SEMAPHORES = ["pe", "act", "dve", "pool", "sent", "out", "ld0", "ld1", "ld2", "ld3", "ld4", "ld5", "ld6"] + \
    ["rv%d_%d" % (m, h) for m in range(3) for h in range(NS)] + ["rt%d" % m for m in range(3)]
IO = {"ends", "db", "wt", "salt", "nz", "sl", "ye", "yv", "yp"}
CACHE = {}


def span(ap):
    name, idx = ap[0], ap[1]
    if name in IO:
        return None
    shape = SCRATCH[name][1]
    key = (name, str(idx))
    if key not in CACHE:
        p = np.arange(128)[idx[0]]
        c = np.arange(int(np.prod(shape[1:]))).reshape(shape[1:])[idx[1:]]
        CACHE[key] = (name, int(np.min(p)), int(np.max(p)), int(np.min(c)), int(np.max(c)), int(np.size(c)))
    return CACHE[key]


def build(P):
    ops = []
    tag = [None]
    al = slice(None)

    def ap(name, a=None, b=None, st=None, p=al):
        return (name, (p, slice(a, b, st)))

    def blk(name, j, n=128, p=al):
        return (name, (p, slice(j * n, j * n + n)))

    def apx(name, *idx):
        return (name, idx)

    def n_of(x):
        return span(x)[5]

    def rate(*xs):
        return 0.5 if all(SCRATCH[x[0]][2] in (S_, U_) for x in xs) else 1

    def add(eng, kind, args, reads, writes, cost, **kw):
        op = {"eng": eng, "kind": kind, "args": args, "reads": [span(r) for r in reads if span(r)],
              "writes": [span(w) for w in writes if span(w)], "cost": cost, "id": len(ops), "tag": tag[0]}
        op.update(kw)
        ops.append(op)
        return op

    def aps(*xs):
        return [x for x in xs if isinstance(x, tuple)]

    def ts(out, in0, s1, s2, op0, op1=None):
        add("dve", "ts", (out, in0, s1, s2, op0, op1), aps(in0, s1, s2), [out], max(64, n_of(out) * rate(out, in0)))

    def tt(out, in0, in1, op):
        ps = in0[0][:2] == "ps" or in1[0][:2] == "ps"
        add("dve", "tt", (out, in0, in1, op), [in0, in1], [out], max(64, n_of(out) * (1 if ps else 2)))

    def cp(out, in_):
        add("dve", "cp", (out, in_), [in_], [out], max(64, n_of(out) * rate(out, in_)))

    def ms(out, v):
        add("dve", "ms", (out, v), [], [out], max(64, n_of(out) * rate(out)))

    def scan(out, a, b, op0, op1):
        add("dve", "scan", (out, a, b, op0, op1), [a, b], [out], max(64, n_of(out) * rate(out, a, b)))

    def act(out, in_, f, bias=0.0, scale=1.0):
        add("act", "act", (out, in_, f, bias, scale), aps(in_, bias, scale), [out], max(64, n_of(out)))

    def mm(*grps, ends=(True, True), also=()):
        rd, wr, c = [], [], 0
        lst = [x for grp in grps for x in grp]
        for (o, l, r) in lst:
            rd += [l, r]
            wr.append(o)
            c += max(min(64, n_of(l)), n_of(r)) * (4 if SCRATCH[l[0]][2] == F_ else 1)
        add("pe", "mm", (lst, grps, ends), rd + list(also), wr, c * P["pe"] + 30)

    def iota(out, pat, base, cm):
        add("pool", "iota", (out, pat, base, cm), [], [out], 160 + 2 * n_of(out))

    def gather(eng, out, win, off):
        add(eng, "gat", (out, win, off), [win, off], [out], 70 + n_of(out) * P["g"])

    def dma(q, out, in_, sem, lat):
        add(q, "dma", (out, in_, sem), [in_], [out], 60, lat=lat, sem=sem)

    def send(src, dst, to, sem, lat):
        s = add("pool", "send", (src, dst, to, sem), [src], [], 600, lat=0.0)
        add("net", "arrive", (sem,), [], [dst], 0, lat=lat, after=s["id"], sem=sem)

    def c_(j):
        return ap("col", j, j + 1)

    def q32(b):
        return slice(32 * b, 32 * b + 32)

    p8 = slice(0, 8)
    dma("sp", ap("e_in"), ap("ends"), "ld0", 2000)
    dma("act", ap("wt_in"), ap("wt"), "ld1", 2000)
    dma("act", ap("salt_in"), ap("salt"), "ld2", 2200)
    dma("sp", ap("win", 0, W), ap("db"), "ld3", P["db"])
    dma("act", ap("nz_in", 0, 128), ap("nz", 0, 128), "ld4", 2400)
    dma("sp", ap("nz_in", 128, 1536), ap("nz", 128, 1536), "ld6", P["db"] + 1500)
    dma("act", ap("sl_in", p=p8), ap("sl"), "ld5", 2500)

    iota(ap("pk", 0, 1), [[0, 1]], 0, 1)
    iota(ap("nN"), [[1, 128]], 0, 0)
    iota(ap("nG"), [[1, 8], [0, 16]], 0, 0)
    iota(ap("nI"), [[0, 8], [1, 16]], 0, 0)
    iota(ap("n8"), [[1, 8]], 0, 0)
    iota(ap("n32"), [[1, 32]], 0, 0)
    iota(ap("nJ"), [[0, 8], [1, 32]], 0, 0)
    ts(ap("pk", 1, 2), ap("pk", 0, 1), 4, None, A.arith_shift_right)
    ts(ap("pk", 2, 3), ap("pk", 0, 1), 15, None, A.bitwise_and)
    cp(ap("col", 0, 3), ap("pk", 0, 3))
    ts(c_(3), c_(2), 15.0, None, A.is_equal)
    ts(blk("ee", 0), ap("e_in"), c_(3), None, A.add)
    send(blk("ee", 0), blk("vin", 0), +1, "rv0_0", P["rem"] + 2000)
    send(blk("ee", 0), blk("tin", 0), -1, "rt0", P["rem"])
    ts(c_(4), c_(2), 15.0, None, A.not_equal)
    ts(c_(5), c_(4), 0.25, None, A.mult)
    ts(c_(6), c_(4), 0.5, None, A.mult)
    ts(c_(7), c_(3), 0.875, 0.5, A.mult, A.add)
    ts(c_(8), c_(3), -0.375, None, A.mult)
    ts(c_(9), c_(3), -31.5, None, A.mult)
    ts(c_(10), c_(2), -2.0, 1.0, A.mult, A.add)
    ts(c_(11), c_(2), 1.0, None, A.is_equal)
    ts(c_(12), c_(2), 2.0, None, A.is_lt)
    ts(c_(13), c_(2), 0.0, None, A.is_equal)
    ts(c_(14), c_(1), 4.0, None, A.mult)
    ts(c_(15), c_(0), float(W), 2.0 ** -15, A.add, A.mult)
    ts(ap("gcol"), ap("n8"), c_(1), None, A.is_equal)
    ts(ap("wt2"), ap("wt_in"), c_(9), 1.0 / 64, A.add, A.mult)
    for g in range(8):
        ts(blk("mW", g, 16), ap("wt2"), ap("gcol", g, g + 1), None, A.mult)
    ts(ap("mI"), ap("nN"), c_(0), None, A.is_equal)
    ts(ap("mBO"), ap("nG"), c_(1), None, A.is_equal)
    act(ap("mI128"), ap("mI"), AF.Copy, scale=-128.0)
    act(ap("mIb"), ap("mI"), AF.Copy, scale=65536.0)
    act(ap("mIn"), ap("mI"), AF.Copy, scale=-1.0)
    act(ap("mIc"), ap("mI"), AF.Identity, scale=c_(4))
    act(ap("mH4"), ap("mI"), AF.Identity, scale=c_(5))
    act(ap("mF2"), ap("mI"), AF.Identity, scale=c_(6))
    act(blk("tmp", 0), ap("mI"), AF.Identity, scale=c_(7))
    act(blk("tmp", 1), ap("mBO"), AF.Identity, scale=c_(8))
    tt(ap("mV2"), blk("tmp", 0), blk("tmp", 1), A.add)
    ms(ap("mT", 128, 144), 0.0)
    act(blk("mT", 0), ap("mI"), AF.Identity, scale=c_(3))
    ts(blk("tmp", 2), ap("nN"), c_(0), -2.0, A.is_gt, A.mult)
    tt(blk("tmp", 2), blk("tmp", 2), ap("mBO"), A.mult)
    tt(ap("mL"), blk("tmp", 2), ap("mI"), A.add)
    for k in range(4):
        cp(apx("sd", al, al, k, al), ap("salt_in", k, 128, 4))
    cp(apx("sd", al, al, slice(4, 8), al), apx("sd", al, al, slice(0, 4), al))
    for s in range(4):
        act(apx("sd8", al, slice(s * NS, s * NS + NS), al, al), apx("sd", al, al, al, al), AF.Identity,
            bias=float(8 * (211 * s - 2738)), scale=8.0)
    ms(ap("rs0"), 1.0)
    ms(ap("rs0", 0, None, 16), 0.0)
    ms(ap("rs1"), 0.0)
    ms(ap("rs1", 0, None, 16), 256.0)
    ms(ap("d0"), 2.0)
    ms(ap("win", W, FB), 0.0)
    ms(ap("ones"), 1.0)
    ts(apx("fi", al, al, slice(AC, NB)), ap("ones"), c_(13), None, A.mult)
    for st in range(12):
        k0 = (st % 4 - st // 4) % 4
        for h in range(NS):
            base = 16384 - (FB + 128 * st + NB * h)
            for (r0, r1) in ((0, 3 - k0), (3 - k0, 3)):
                if r1 > r0:
                    iota(apx("d1", al, st * NS + h, slice(2 * B * r0, 2 * B * r1, 2)), [[-1, r1 - r0], [-4, B]],
                         base - (k0 + 1 + r0) % 4, 0)
        v = apx("d1", al, slice(st * NS, st * NS + NS), slice(0, 2 * AC, 2))
        act(v, v, AF.Copy, scale=2.0 ** -15)
    cp(ap("slf", p=p8), ap("sl_in", p=p8))
    ts(ap("mG", p=p8), ap("nG", p=p8), ap("col", 0, 1, p=p8), None, A.is_equal)
    ts(blk("tmp", 3), ap("nI"), 15.0, None, A.is_equal)
    tt(ap("mR15"), blk("tmp", 3), ap("mBO"), A.mult)
    act(ap("mBf"), ap("mBO"), AF.Copy, scale=32768.0)
    ts(ap("rcol", 0, 8), ap("gcol"), c_(12), None, A.mult)
    ts(ap("rcol", 8, 16), ap("rcol", 0, 8), -1.0, None, A.mult)
    for j in range(16):
        ts(blk("mR", j, 32), blk("ones", 0, 32), ap("rcol", j, j + 1), None, A.mult)
    ts(ap("mRR"), ap("mBO"), c_(12), -(2.0 ** -15), A.mult, A.mult)
    for s in range(4):
        ts(blk("tmp", 4 + s, 32), ap("n32"), c_(14), float(s), A.subtract, A.is_equal)
    ts(ap("mY"), blk("tmp", 1), c_(12), None, A.mult)
    act(ap("mYf"), blk("tmp", 1), AF.Copy, scale=32768.0)
    ts(ap("pk", 3, 4), ap("pk", 0, 1), 31, None, A.bitwise_and)
    cp(c_(16), ap("pk", 3, 4))
    ts(ap("mTri"), ap("nJ"), c_(16), 0.5, A.is_le, A.mult)
    ts(ap("mTr"), ap("nI"), c_(2), c_(15), A.is_equal, A.mult)
    ts(ap("mTr"), ap("mTr"), -1.5, None, A.add)
    act(ap("mA"), ap("gcol"), AF.Copy, scale=32768.0)

    M2 = 1.5 * 2.0 ** 23
    bS, bX, bE = "ps4", "ps5", ("ps6", "ps7")
    mI, mIn, mBO = ap("mI"), ap("mIn"), ap("mBO")
    for m in range(3):
        last = m == 2
        gv = P["gv"][1 if last else 0]
        for h in range(NS):
            hp = slice(NB * h, NB * h + NB)
            e, t, aB = blk("ee", NS * m + h, NB), blk("tin", NS * m + h, NB), blk("aB", h, NB)
            o = ap(bS, 384, 384 + NB)
            mm([(o, mI, e), (o, mIn, t)])
            act(aB, o, AF.Abs)
            sl = blk("slf", NS * m + h, NB, p=p8)
            mm([(o, mBO, aB), (o, ap("mG", p=p8), sl)])
            act(blk("bs", h, NB), o, AF.Copy)
            if not last:
                o = blk(bS, 3, p=hp)
                mm([(o, aB, mBO), (o, sl, ap("mG", p=p8))])
                act(ap("bsT", p=hp), o, AF.Copy)
        if last:
            ts(ap("e0"), blk("ee", 2), c_(3), None, A.subtract)
        for s in range(4):
            k0, st, par = (s - m) % 4, 4 * m + s, s % 2
            kk = [(k0 + 1 + r) % 4 for r in range(4)]
            for h in range(NS):
                tag[0] = (st, h)
                c0, y = NB * h, par * NS + h
                vb, vo = ("vin", 128 * m + c0) if s == 0 else ("vv", 128 * (st - 1) + c0)
                b0, b1 = "ps%d" % (2 * h), "ps%d" % (2 * h + 1)
                mm(*[[(blk(b0, r, B), ap("mW"), ap(vb, vo + kk[r], vo + NB, 4))] for r in range(4)])
                uu, q, zz, pl, ui = blk("uu", y, NB), blk(b1, 0, NB), blk("zz", y, NB), blk("pl", y, NB), blk("ui", y, NB)
                act(uu, blk(b0, 0, NB), AF.Identity, bias=M2)
                act(q, uu, AF.Square, bias=148 - M2)
                tt(zz, q, apx("sd8", al, s * NS + h, slice(k0 + 1, k0 + 5), al), A.add)
                ts(pl, zz, 3, W - 1, A.arith_shift_right, A.bitwise_and)
                x0 = y * AC
                cp(blk("of1", y, AC), ap("pl", y * NB, y * NB + AC))
                ts(apx("d1", al, st * NS + h, slice(1, 2 * NB, 2)), pl, -(2.0 ** -15), 0.5, A.mult, A.add)
                ts(ui, uu, M2, None, A.subtract)
                ts(apx("ask", al, s * NS + h, al), ui, 7, None, A.bitwise_and)
                v, nz, mb = ap(vb, vo, vo + NB), blk("nz_in", st * NS + h, NB), blk("mb", y, NB)
                t1, t2 = blk(bX, h, NB), blk(bX, 2 * NS + h, NB)
                mm([(t1, mI, v), (t1, mI, nz)])
                act(mb, t1, AF.Sign, bias=-255.5)
                mm([(t2, mI, v), (t2, mI, nz), (t2, ap("mI128"), mb)])
                f0 = FB + 128 * st + c0
                act(ap("win", f0, f0 + NB), t2, AF.Identity, bias=-128.0)
                for (eng, a, b) in (("act", 0, AC - gv[0]), ("dve", AC - gv[0], AC)):
                    if b > a:
                        gather(eng, ap("got", 16 * (x0 + a), 16 * (x0 + b)), ap("win", 0, W), ap("of1", x0 + a, x0 + b))
                tg = ap(b0, NB, NB + AC)
                mm([(tg, ap("mT", 15 - p, 143 - p), ap("got", 16 * x0 + p, 16 * (x0 + AC), 16)) for p in range(16)])
                hit = ap("d0", 2 * x0 + 1, 2 * (x0 + AC), 2)
                tt(hit, tg, apx("ask", al, s * NS + h, slice(0, AC)), A.is_equal)
                scan(blk("o2", y, 2 * AC), blk("d0", y, 2 * AC), apx("d1", al, st * NS + h, slice(0, 2 * AC)), A.max, A.min)
                ts(blk("of2", y, AC), ap("o2", 2 * x0 + 1, 2 * (x0 + AC), 2), -32768.0, 16384.0, A.mult, A.add)
                for (eng, a, b) in (("act", 0, AC - gv[1]), ("dve", AC - gv[1], AC)):
                    if b > a:
                        xx = ap("xx", 16 * (x0 + a), 16 * (x0 + b))
                        gather(eng, xx, ap("win", 0, f0 + NB), ap("of2", x0 + a, x0 + b))
                        scan(ap("smx", 16 * (x0 + a), 16 * (x0 + b)), ap("rs0", 0, 16 * (b - a)), xx, A.mult, A.max)
                        scan(ap("smn", 16 * (x0 + a), 16 * (x0 + b)), ap("rs1", 0, 16 * (b - a)), xx, A.add, A.min)
                vs0 = 2 * NB
                mm([(blk(b0, 2, NB), ap("mV2"), v),
                    (ap(b0, vs0 + k0, vs0 + NB, 4), ap("mF2"), ap("win", f0 + k0, f0 + NB, 4))], ends=(True, False), also=[hit])
                for nm in ("smx", "smn"):
                    mm([(ap(b0, vs0 + kk[r], vs0 + NB, 4), ap("mH4"), ap(nm, 16 * (x0 + B * r) + 15, 16 * (x0 + B * r + B), 16))
                        for r in range(3)], ends=(False, nm == "smn"))
                ts(blk("vv", st * NS + h, NB), blk(b0, 2, NB), M2, M2, A.add, A.subtract)
                w = ap(b1, NB, NB + AC)
                mm([(w, ap("mL"), hit)])
                act(apx("fi", al, s * NS + h, slice(0, AC)), w, AF.Relu, bias=c_(10), scale=-1.0)
            tag[0] = (st, -1)
            hs = slice(s * NS, s * NS + NS)
            for r in range(4):
                fi = apx("fi", al, hs, slice(B * r, B * r + B))
                tt(ap("pP", 128 * s + kk[r], 128 * s + 128, 4), fi,
                   apx("d1", al, slice(st * NS, st * NS + NS), slice(2 * B * r + 1, 2 * B * r + 2 * B, 2)), A.mult)
                if not last:
                    tt(ap("pA", 128 * par + kk[r], 128 * par + 128, 4), fi, apx("ask", al, hs, slice(B * r, B * r + B)), A.mult)
            if not last:
                gg, ff = blk("gg", par), blk("ff", s)
                mm([(blk(bS, 0), ap("mBf"), blk("pP", s))])
                act(gg, blk(bS, 0), AF.Identity, scale=c_(11))
                tt(ff, blk(bS, 0), gg, A.subtract)
                o = blk(bS, 2)
                mm([(o, ap("mIc"), ap("win", FB + 128 * st, FB + 128 * st + 128)), (o, ap("mR15"), blk("pA", par))])
                act(blk("rec", s), o, AF.Copy)
                d, o = blk(bE[par], 0, 256), blk("eq", s, 256)
                mm([(d, ff, blk("mR", 0, 256))] + [(d, ap("mIb"), ap("mTri"))] * P["ea"], ends=(True, False))
                for b in range(4):
                    mm([(blk(bE[par], g, 32, p=q32(b)), blk("mR", 8 + g, 32), blk("ff", 4 * s + b, 32)) for g in range(8)],
                       ends=(False, True))
                if P["ea"]:
                    act(o, d, AF.Abs)
                    act(o, o, AF.Relu, bias=1.0, scale=-1.0)
                else:
                    tt(o, d, ap("mTri"), A.is_equal)
        tag[0] = None
        o = blk(bS, 0, p=q32(0))
        mm([(o, blk("mYf" if last else "mY", s, 32), blk("pP" if last else "ff", s)) for s in range(4)])
        act(ap("ypa", p=q32(0)), o, AF.Abs, bias=-8192.5)
        act(blk("ypb", m, p=q32(0)), ap("ypa", p=q32(0)), AF.Identity, bias=8191.5, scale=-1.0)
        dma("sp", blk("yp", m, 512), blk("ypb", m, p=q32(0)), "out", 2000)
        for h in range(NS):
            hp = slice(NB * h, NB * h + NB)
            b0, b1 = "ps%d" % (2 * h), "ps%d" % (2 * h + 1)
            v, e, t = blk("vv", (4 * m + 3) * NS + h, NB), blk("ee", NS * m + h, NB), blk("tin", NS * m + h, NB)
            d, dv, av, aA = blk(b1, 0, NB), blk(b0, 0, NB), blk(b1, 1, NB), blk("aA", h, NB)
            mm([(d, mI, v), (d, mIn, t)])
            mm([(dv, mI, v), (dv, mIn, e)])
            act(aA, d, AF.Abs)
            mm([(av, mBO, aA)])
            ok, en = blk("okf", NS * m + h, NB), blk("ee", NS * (m + 1) + h, NB)
            tt(ok, av, blk("bs", h, NB), A.is_le)
            tt(blk("prod", h, NB), dv, ok, A.mult)
            tt(en, blk("prod", h, NB), blk("e0", h, NB) if last else e, A.add)
            if not last:
                send(en, blk("vin", NS * (m + 1) + h, NB), +1, "rv%d_%d" % (m + 1, h), P["rem"])
                o = blk(bX, 1, p=hp)
                mm([(o, aA, mBO)])
                tt(ap("okT", p=hp), o, ap("bsT", p=hp), A.is_le)
        dma("sp", blk("yv", m), blk("okf", m, p=slice(0, 128, 16)), "out", 2000)
        if last:
            dma("act", ap("ye"), blk("ee", 3), "out", 2000)
            continue
        send(blk("ee", m + 1), blk("tin", m + 1), -1, "rt%d" % (m + 1), P["rem"])
        for s in range(4):
            zb = bE[s % 2]
            mm([(blk(zb, 0), blk("ff", s), ap("mRR")), (blk(zb, 0), mIn, ap("okT"))], ends=(True, False))
            mm(*[[(blk(zb, g, 16, p=q32(b)), blk("eq", 8 * s + g, 32, p=q32(b)), blk("okT", g, 16, p=q32(b)))
                  for g in range(8)] for b in range(4)], ends=(False, True))
            tt(blk("x2", s), blk(zb, 0), ap("mTr"), A.min)
            mm([(blk(bS, s, 8), blk("x2", s), ap("mA"))])
            ts(blk("ofs", s, 8), blk(bS, s, 8), 1.5 * 16 * 32768, None, A.add)
            for b in (3, 2, 1, 0):
                add("dve", "sca", (ap("win", 0, FB), blk("ofs", 4 * s + b, 2), blk("rec", 4 * s + b, 32)),
                    [blk("ofs", 4 * s + b, 2), blk("rec", 4 * s + b, 32)], [ap("win", 0, FB)], 60 + 32 * P["sc"])
    return ops


def depends(ops):
    seen = {}
    for op in ops:
        d = set()
        for (acc, wr) in [(r, False) for r in op["reads"]] + [(w, True) for w in op["writes"]]:
            for (o, p0, p1, a, b, w2) in seen.get(acc[0], []):
                if (wr or w2) and p0 <= acc[2] and acc[1] <= p1 and a <= acc[4] and acc[3] <= b:
                    d.add(o)
        if "after" in op:
            d.add(op["after"])
        op["deps"] = d
        for acc in op["writes"]:
            full = acc[5] == acc[4] - acc[3] + 1
            seen[acc[0]] = [x for x in seen.get(acc[0], [])
                            if not (full and acc[1] <= x[1] and x[2] <= acc[2] and acc[3] <= x[3] and x[4] <= acc[4])]
        for (acc, wr) in [(r, False) for r in op["reads"]] + [(w, True) for w in op["writes"]]:
            seen.setdefault(acc[0], []).append((op["id"], acc[1], acc[2], acc[3], acc[4], wr))
        op["banks"] = sorted(set(a[0] for a in op["reads"] + op["writes"] if a[0][:2] == "ps"))


def in_line(ops, i, j):
    return ops[i]["eng"] == "pe" and ops[j]["eng"] == "pe"


def schedule(ops, P):
    hop, n = P["hop"], len(ops)
    succ = [[] for _ in range(n)]
    for op in ops:
        for d in op["deps"]:
            succ[d].append((op["id"], 0.0 if in_line(ops, d, op["id"]) else hop))
    dur = [op["cost"] * 1.04 for op in ops]
    prio = [0.0] * n
    for i in range(n - 1, -1, -1):
        prio[i] = dur[i] + ops[i].get("lat", 0.0) + max([prio[j] + gp for (j, gp) in succ[i]] + [0.0])
    for i in range(n):
        tg = ops[i]["tag"]
        prio[i] -= (P["skew"] * tg[1] if tg[1] >= 0 else P["off"]) if tg else 0.0
        prio[i] += P["lift"] if ops[i]["kind"] == "sca" or (ops[i]["kind"] != "mm" and ops[i]["args"][0][0] in LIFT) else 0.0
    left = [len(op["deps"]) for op in ops]
    ready = [i for i in range(n) if left[i] == 0]
    done, base, free, lastb, order = [0.0] * n, [0.0] * n, {}, {}, []
    while ready:
        est = {}
        for i in ready:
            op = ops[i]
            t = max(base[i], free.get(op["eng"], 0.0))
            for bk in op["banks"]:
                for (e, j) in lastb.get(bk, {}).items():
                    if e != op["eng"]:
                        t = max(t, done[j] + hop)
            est[i] = t
        t0 = min(est.values())
        e0 = ops[min(ready, key=lambda i: (est[i], -prio[i], i))]["eng"]
        i = max([j for j in ready if ops[j]["eng"] == e0 and est[j] <= t0 + P["delta"]], key=lambda j: (prio[j], -j))
        for bk in ops[i]["banks"]:
            lastb.setdefault(bk, {})[e0] = i
        if e0 != "net":
            free[e0] = est[i] + dur[i]
        done[i] = est[i] + dur[i] + ops[i].get("lat", 0.0)
        order.append(i)
        ready.remove(i)
        for (j, gp) in succ[i]:
            base[j] = max(base[j], done[i] + gp)
            left[j] -= 1
            if left[j] == 0:
                ready.append(j)
    return order


def improve(ops, order, P, its):
    n = len(ops)
    anc, pred = [0] * n, []
    for i in range(n):
        ds = ops[i]["deps"]
        for d in ds:
            anc[i] |= anc[d] | (1 << d)
        pred.append([d for d in sorted(ds) if not any(anc[x] >> d & 1 for x in ds)])
    eng, banks = [op["eng"] for op in ops], [op["banks"] for op in ops]
    cases = []
    for c in P["cases"]:
        alt = build(dict(P, **c))
        dur = [(o["cost"] + (c["fix"] if o["eng"] in ("act", "dve") else 0)) * 1.04 for o in alt]
        gaps = [[(d, alt[d].get("lat", 0.0) + (0.0 if in_line(ops, d, i) else c["hop"])) for d in pred[i]] for i in range(n)]
        cases.append((dur, gaps, c["hop"], [o.get("lat", 0.0) for o in alt]))

    def run(order, case):
        dur, gaps, hop, lat = case
        fin, why, last, lastb = [0.0] * n, [-1] * n, {}, {}
        for i in order:
            e = eng[i]
            w = last.get(e, -1) if e != "net" else -1
            t = fin[w] if w >= 0 else 0.0
            for (d, gp) in gaps[i]:
                if fin[d] + gp > t:
                    t, w = fin[d] + gp, d
            for bk in banks[i]:
                lb = lastb.setdefault(bk, {})
                for e2 in lb:
                    if e2 != e and fin[lb[e2]] + hop > t:
                        t, w = fin[lb[e2]] + hop, lb[e2]
                lb[e] = i
            fin[i], why[i], last[e] = t + dur[i], w, i
        end = max(range(n), key=lambda i: fin[i] + lat[i])
        return fin[end] + lat[end], why, end

    rng = np.random.default_rng(1)
    rs = [run(order, c) for c in cases]
    cur = sum(r[0] for r in rs)
    best = (cur, order)
    for it in range(its):
        _, why, v = rs[it % len(rs)]
        arcs = []
        while why[v] >= 0:
            if not anc[v] >> why[v] & 1:
                arcs.append((why[v], v))
            v = why[v]
        if not arcs:
            break
        u, v = arcs[int(rng.integers(len(arcs)))]
        a, b = order.index(u), order.index(v) + 1
        seg = order[a:b]
        if rng.random() < 0.5:
            front = [x for x in seg if x == v or anc[v] >> x & 1]
        else:
            front = [x for x in seg if x != u and not anc[x] >> u & 1]
        fs = set(front)
        new = order[:a] + front + [x for x in seg if x not in fs] + order[b:]
        r2 = [run(new, c) for c in cases]
        t = sum(r[0] for r in r2)
        if t <= cur + P["heat"] * (1 - it / its) * rng.random():
            cur, rs, order = t, r2, new
            if t < best[0]:
                best = (t, new)
    return best


def plan():
    if "plan" not in CACHE:
        best = None
        for alt in TRY:
            P = dict(PARAM, **alt)
            ops = build(P)
            depends(ops)
            t, order = improve(ops, schedule(ops, P), P, P["few"])
            if best is None or t < best[0]:
                best = (t, order, ops, alt)
        PARAM.update(best[3])
        ops = best[2]
        order = improve(ops, best[1], PARAM, PARAM["many"])[1]
        place = {i: x for (x, i) in enumerate(order)}
        count, clock, stamp, lastb, out = {}, {}, {}, {}, []
        for i in order:
            op = ops[i]
            if op["kind"] == "arrive":
                stamp[i] = (op["sem"], "all", {})
                continue
            ds = set(d for d in op["deps"] if not in_line(ops, d, i))
            for bk in op["banks"]:
                ds.update(j for (e, j) in lastb.get(bk, {}).items() if e != op["eng"])
                lastb.setdefault(bk, {})[op["eng"]] = i
            known = clock.setdefault(op["eng"], {})
            waits = {}
            for d in sorted(ds, key=lambda d: -place[d]):
                sem, val, past = stamp[d]
                if known.get(sem, 0) == "all" or (val != "all" and known.get(sem, 0) >= val):
                    continue
                waits[sem] = val
                known[sem] = val
                for (k, x) in past.items():
                    if x == "all" or (known.get(k, 0) != "all" and x > known.get(k, 0)):
                        known[k] = x
            if op["kind"] == "dma":
                stamp[i] = (op["sem"], 16, dict(known))
            elif op["kind"] != "send":
                count[op["eng"]] = count.get(op["eng"], 0) + 1
                stamp[i] = (op["eng"], count[op["eng"]], dict(known))
            out.append((op, waits))
        CACHE["plan"] = (out, count, best[0])
    return CACHE["plan"]


def rank_program(g, core, T, topo):
    rank = T.rank_of(core)
    if rank is None:
        return
    n = len(T.cores)
    peer = {d: T.cores[(rank + d) % n] for d in (1, -1)}
    lanes_in = {"rv": len(topo.engines(peer[-1], core)), "rt": len(topo.engines(peer[1], core))}
    Q = {"pe": g.tensor, "act": g.scalar, "dve": g.vector, "pool": g, "sp": g.sync}
    calls, count, _ = plan()

    def R(x):
        return T[x[0]][x[1]] if isinstance(x, tuple) else x

    sent, outs = 0, 0
    for (op, waits) in calls:
        q, k, a = Q[op["eng"]], op["kind"], op["args"]
        for (sem, val) in waits.items():
            q.wait_ge(T.sem[sem], lanes_in[sem[:2]] if val == "all" else val)
        if k == "dma":
            q.dma_start(R(a[0]), R(a[1])).then_inc(T.sem[a[2]], 16)
            outs += 16 if a[2] == "out" else 0
            continue
        if k == "send":
            dst = peer[a[2]]
            rid, pid = topo.addr(dst)[:2]
            g.remote_dma(R(a[1]), R(a[0]), T.sem[a[3]], T.sem["sent"], pid, rid, topo.mask(core, dst))
            sent += len(topo.engines(core, dst))
            continue
        if k == "ts":
            ins = q.tensor_scalar(R(a[0]), R(a[1]), R(a[2]), R(a[3]), *[x for x in a[4:] if x is not None])
        elif k == "tt":
            ins = q.tensor_tensor(R(a[0]), R(a[1]), R(a[2]), a[3])
        elif k == "cp":
            ins = q.tensor_copy(R(a[0]), R(a[1]))
        elif k == "ms":
            ins = q.memset(R(a[0]), a[1])
        elif k == "scan":
            ins = q.tensor_tensor_scan(R(a[0]), R(a[1]), R(a[2]), 0.0, a[3], a[4])
        elif k == "act":
            ins = q.activation(R(a[0]), R(a[1]), a[2], R(a[3]), R(a[4]))
        elif k == "iota":
            if SCRATCH[a[0][0]][2] == I_:
                ins = q.iota(R(a[0]), a[1], a[2], a[3])
            else:
                ins = q.iota(R(a[0]), a[1], a[2], a[3], allow_small_or_imprecise_dtypes=True)
        elif k == "gat":
            src = R(a[1]).indirect(R(a[2]))
            ins = q.activation(R(a[0]), src, AF.Copy) if op["eng"] == "act" else q.tensor_copy(R(a[0]), src)
        elif k == "sca":
            ins = q.tensor_copy(R(a[0]).indirect(R(a[1])), R(a[2]))
        else:
            for lst in a[1]:
                for j in range(len(lst)):
                    ins = q.matmul(R(lst[j][0]), R(lst[j][1]), R(lst[j][2]), a[2][0] and j == 0, a[2][1] and j == len(lst) - 1)
        ins.then_inc(T.sem[op["eng"]], 1)
    for e in ("pe", "act", "dve", "pool"):
        g.sync.wait_ge(T.sem[e], count[e])
    g.sync.wait_ge(T.sem["out"], outs)
    g.wait_ge(T.sem["sent"], sent)
